import numpy as np
import ml_dtypes


def mxq(x, axis, fmt="e4m3"):
    dtype, down = {"e4m3": (ml_dtypes.float8_e4m3fn, 7), "e5m2": (ml_dtypes.float8_e5m2, 14)}[fmt]
    v = np.moveaxis(np.asarray(x, np.float32).astype(ml_dtypes.bfloat16).astype(np.float64), axis, -1)
    blocks = v.reshape(v.shape[:-1] + (-1, 32))
    amax = np.abs(blocks).max(-1, keepdims=True)
    byte = np.maximum(np.where(amax > 0, np.frexp(amax)[1] - 1 + 127, 0) - down, 1)
    scale = np.exp2(byte - 127.0)
    codes = (blocks / scale).astype(np.float32).astype(dtype).astype(np.float64)
    return np.moveaxis((codes * scale).reshape(v.shape), -1, axis)


WIDE = False


def mx_kscale(k):
    if not WIDE:
        return np.ones(k)
    levels = np.array([10, -10, 5, -5, 0])
    if k % 512:
        return np.exp2(np.random.permutation(np.resize(levels, k // 32))).repeat(32)
    a = np.empty((k // 512, 16))
    for p in range(k // 512):
        a[p, :8] = np.random.permutation(np.resize(levels, 8))
        for g in range(8):
            far = levels[np.abs(levels - a[p, g]) >= 10]
            a[p, g + 8] = far[np.random.randint(len(far))]
    return np.exp2(a.ravel()).repeat(32)


def f64(x):
    return np.asarray(x).astype(np.float64)


def striped(idx):
    return np.tile(idx.reshape(-1, 16).T, (8, 1)).astype(np.uint16)


def unstriped(offs):
    return offs[:16].T.reshape(-1).astype(np.int64)


E2M1 = np.array([0.0, 0.5, 1.0, 1.5, 2.0, 3.0, 4.0, 6.0, -0.0, -0.5, -1.0, -1.5, -2.0, -3.0, -4.0, -6.0])


def pack_weight(w, fmt):
    k, n = w.shape
    w = f64(np.asarray(w, np.float32).astype(ml_dtypes.bfloat16)).reshape(k // 32, 32, n)
    amax = np.abs(w).max(1)
    if fmt == "e4m3":
        byte = np.frexp(amax)[1] - 1 + 127 - 7
    else:
        mant, ex = np.frexp(amax / 6.0)
        byte = np.where(mant > 0.5, ex, ex - 1) + 127
    byte = np.clip(np.where(amax > 0, byte, 1), 1, 254)
    scaled = (w * np.exp2(127.0 - byte)[:, None, :]).reshape(k, n).astype(np.float32)
    by_word = np.ascontiguousarray(scaled.reshape(k // 512, 128, 4, n).transpose(0, 1, 3, 2))
    if fmt == "e4m3":
        words = by_word.astype(ml_dtypes.float8_e4m3fn).view(np.uint8)
    else:
        c = by_word.astype(ml_dtypes.float4_e2m1fn).view(np.uint8) & 0xF
        words = (c[..., 0::2] | (c[..., 1::2] << 4)).reshape(k // 512, 128, 2 * n)
    return np.ascontiguousarray(words), np.ascontiguousarray(byte.astype(np.uint8).reshape(k // 512, 16, n))


def unpack_weight(words, scales, fmt):
    g, _, n = scales.shape
    words = np.ascontiguousarray(words).reshape(g, 128, n, -1)
    if fmt == "e4m3":
        vals = words.view(ml_dtypes.float8_e4m3fn).astype(np.float64)
    else:
        nib = np.empty((g, 128, n, 4), np.uint8)
        nib[..., 0::2] = words & 0xF
        nib[..., 1::2] = words >> 4
        vals = E2M1[nib]
    vals = vals * np.repeat(np.exp2(scales.astype(np.float64) - 127.0), 8, axis=1)[..., None]
    return vals.transpose(0, 1, 3, 2).reshape(g * 512, n)


K, T, E, C, N = 1536, 512, 4, 256, 512
M = 384


def by_expert(wq, xq):
    return np.concatenate([wq[e].T @ xq[:, e * C:(e + 1) * C] for e in range(E)], axis=1)


def setup_inputs():
    n = np.random.standard_normal
    s = mx_kscale(K)[:, None]
    v = mx_kscale(N)
    first = np.random.permutation(np.repeat(np.arange(E), T // E))
    second = (first + 1 + np.random.permutation(np.repeat(np.arange(E - 1), -(-T // (E - 1)))[:T])) % E
    while np.bincount(second, minlength=E).max() != T // E:
        load = np.bincount(second, minlength=E); hi, lo = int(load.argmax()), int(load.argmin())
        t = np.flatnonzero((second == hi) & (first != lo))[0]; second[t] = lo
    slot_token = np.empty(E * C, np.int64); pos = np.empty((2, T), np.int64); fill = np.zeros(E, np.int64)
    place = np.stack([np.random.permutation(C) for _ in range(E)])
    for r, deal in enumerate((first, second)):
        for t in np.random.permutation(T):
            e = deal[t]; j = e * C + place[e, fill[e]]; fill[e] += 1; slot_token[j] = t; pos[r, t] = j
    g = np.random.uniform(0.2, 0.8, T)
    w = [pack_weight(m, "e2m1") for m in n((E, K, N)) / np.sqrt(K) / s[None] * v[None, None, :]]
    return {
        "xT": (n((K, T)) * s).astype(np.float32),
        "w_words": np.stack([m[0] for m in w]),
        "w_scales": np.stack([m[1] for m in w]),
        "b": (0.3 * n((N, E)) * v[:, None]).astype(np.float32),
        "wp": (n((N, M)) / np.sqrt(N) / v[:, None]).astype(np.float32),
        "gate": np.stack([np.tile(g, (N, 1)), np.tile(1.0 - g, (N, 1))]).astype(np.float32),
        "offs": striped(slot_token),
        "pos1": striped(pos[0]),
        "pos2": striped(pos[1]),
    }


def reference(xT, w_words, w_scales, b, wp, gate, offs, pos1, pos2):
    idx = unstriped(offs)
    w = np.stack([unpack_weight(w_words[e], w_scales[e], "e2m1") for e in range(E)])
    xq = mxq(f64(xT)[:, idx], 0, "e4m3")
    y = by_expert(w, xq)
    y = y + np.repeat(f64(b), C, axis=1)
    c = f64(gate[0]) * y[:, unstriped(pos1)] + f64(gate[1]) * y[:, unstriped(pos2)]
    return mxq(f64(wp), 0, "e4m3").T @ mxq(c, 0, "e4m3")

@@ -1,0 +1,243 @@
+from contextlib import ExitStack
+
+import concourse.mybir as mybir
+
+K, T, E, C, N, M = 1536, 512, 4, 256, 512, 384
+P = 128
+A = K // 512
+S = E * C
+H = T // 2
+
+F32 = mybir.dt.float32
+BF16 = mybir.dt.bfloat16
+I32 = mybir.dt.int32
+U32 = mybir.dt.uint32
+U16 = mybir.dt.uint16
+U8 = mybir.dt.uint8
+FP8X4 = mybir.dt.float8_e4m3fn_x4
+FP4X4 = mybir.dt.float4_e2m1fn_x4
+MULT = mybir.AluOpType.mult
+ADD = mybir.AluOpType.add
+IDENTITY = mybir.ActivationFunctionType.Identity
+
+FLOPS = 2 * K * N * S + 2 * N * M * T
+BYTES = 4 * K * T + E * K * N // 2 + E * K * N // 32 + 4 * N * E + 4 * N * M + 8 * T + 2 * P * 128 + 4 * M * T
+
+
+def tile_moe_nxt_lin_bias_kernel(tc, xT, w_words, w_scales, b, wp, gate, offs, pos1, pos2, out):
+    nc = tc.nc
+    with ExitStack() as ctx:
+        keep = ctx.enter_context(tc.tile_pool(name="keep", bufs=1))
+        psum = ctx.enter_context(tc.psum_pool(name="psum", bufs=1))
+
+        offs_sb = keep.tile([P, S // 16], U16, name="offs_sb")
+        pos_sb = [keep.tile([P, T // 16], U16, name="pos_sb%d" % i) for i in range(2)]
+
+        x_raw = [[keep.tile([P, 4, H], F32, name="x_raw%d_%d" % (a, h)) for h in range(2)] for a in range(A)]
+        x_b = [keep.tile([P, T * 4], BF16, name="x_b%d" % a, align_bytes=64) for a in range(A)]
+        x_w = [keep.tile([P, T], U32, name="x_w%d" % a, align_bytes=64) for a in range(A)]
+        x_s = keep.tile([P, T], U8, name="x_s", align_bytes=64)
+        g_w = [keep.tile([P, A * C], U32, name="g_w%d" % e, align_bytes=64) for e in range(E)]
+        g_s = keep.tile([P, S], U8, name="g_s", align_bytes=64)
+        sh_s = [keep.tile([P, S], U8, name="sh_s%d" % a, align_bytes=64) for a in range(1, A)]
+        w_raw = [keep.tile([P, A * 2 * N], U8, name="w_raw%d" % e, align_bytes=64) for e in range(E)]
+        w_per = [keep.tile([P, A * 2 * N], U8, name="w_per%d" % e, align_bytes=64) for e in range(E)]
+        ws_raw = keep.tile([P, E * A * N], U8, name="ws_raw", align_bytes=64)
+        ws_per = keep.tile([P, E * A * N], U8, name="ws_per", align_bytes=64)
+        b_sb = keep.tile([P, 4, E], F32, name="b_sb")
+        wp_raw = keep.tile([P, 4, M], F32, name="wp_raw")
+        wp_b = keep.tile([P, M * 4], BF16, name="wp_b", align_bytes=64)
+        wp_w = keep.tile([P, M], U32, name="wp_w", align_bytes=64)
+        wp_s = keep.tile([P, M], U8, name="wp_s", align_bytes=64)
+        gate_sb = [keep.tile([P, T], F32, name="gate_sb%d" % i) for i in range(2)]
+        y_sb = [keep.tile([P, S], F32, name="y_sb%d" % t) for t in range(4)]
+        parts = [keep.tile([P, 4, T], F32, name="part%d" % i) for i in range(2)]
+
+        def load_x(a, h):
+            src = xT[a * 512 : (a + 1) * 512, h * H : (h + 1) * H]
+            nc.sync.dma_start(x_raw[a][h][:], src.rearrange("(p j) t -> p j t", j=4))
+
+        def load_w(e):
+            nc.sync.dma_start(
+                w_raw[e][:].bitcast(I32).rearrange("p (a n) -> p a n", a=A),
+                w_words[e].bitcast(I32).rearrange("a p n -> p a n"),
+            )
+
+        def load_w_scales():
+            scales = w_scales.bitcast(I32).rearrange("e a q n -> q (e a) n")
+            for q in range(4):
+                nc.sync.dma_start(
+                    ws_raw[32 * q : 32 * q + 4, :].bitcast(I32).rearrange("q (c n) -> q c n", n=N // 4),
+                    scales[4 * q : 4 * q + 4],
+                )
+
+        def cast_x(a, h, engine):
+            dst = x_b[a][:, h * 1024 : (h + 1) * 1024].rearrange("p (t j) -> p t j", j=4)
+            src = x_raw[a][h][:].rearrange("p j t -> p t j")
+            if engine == "v":
+                nc.vector.tensor_copy(dst, src)
+            else:
+                nc.scalar.copy(dst, src)
+
+        def quantize_x(a):
+            nc.vector.quantize_mx(out=x_w[a][:].bitcast(FP8X4), scales=x_s[4 * a : P, :], in_=x_b[a][:])
+
+        def permute_w(e, engine):
+            dst = w_per[e][:].bitcast(I32).rearrange("p (a t q r) -> p a t q r", a=A, t=4, q=16)
+            src = w_raw[e][:].bitcast(I32).rearrange("p (a q t r) -> p a t q r", a=A, t=4, q=16)
+            for a in range(A):
+                engine.tensor_copy(dst[:, a], src[:, a])
+
+        def permute_scales():
+            dst = ws_per[:].bitcast(I32).rearrange("p (c t q r) -> p t c q r", c=E * A, t=4, q=16)
+            src = ws_raw[:].bitcast(I32).rearrange("p (c q t r) -> p t c q r", c=E * A, t=4, q=16)
+            for t in range(4):
+                nc.vector.tensor_copy(dst[:, t], src[:, t])
+
+        def gather(a, e):
+            lists = offs_sb[:, e * 16 : (e + 1) * 16]
+            nc.vector.tensor_copy(g_w[e][:, a * C : (a + 1) * C], x_w[a][:].indirect(lists))
+
+        def gather_scales(e):
+            nc.vector.tensor_copy(g_s[:, e * C : (e + 1) * C], x_s[:].indirect(offs_sb[:, e * 16 : (e + 1) * 16]))
+
+        def shift_scales(e0, e1, queue):
+            for a in range(1, A):
+                for q in range(4):
+                    queue.dma_start(
+                        sh_s[a - 1][32 * q : 32 * q + 4, e0 * C : e1 * C].bitcast(I32),
+                        g_s[32 * q + 4 * a : 32 * q + 4 * a + 4, e0 * C : e1 * C].bitcast(I32),
+                    )
+
+        def expert(e, t):
+            acc = psum.tile([P, C], F32, name="acc", bufs=5)
+            for h in range(2):
+                for a in range(A):
+                    c0 = a * C + h * 128
+                    s0 = (e * A + a) * N + t * 128
+                    g0 = e * C + h * 128
+                    nc.tensor.matmul_mx(
+                        out=acc[:, h * 128 : (h + 1) * 128],
+                        lhsT=w_per[e][:, (a * 4 + t) * 256 : (a * 4 + t + 1) * 256].bitcast(FP4X4),
+                        lhsT_scale=ws_per[:, s0 : s0 + 128],
+                        rhs=g_w[e][:, c0 : c0 + 128].bitcast(FP8X4),
+                        rhs_scale=(g_s if a == 0 else sh_s[a - 1])[:, g0 : g0 + 128],
+                        start=(a == 0),
+                        stop=(a == A - 1),
+                    )
+            if t == 0 and e % 2 == 1:
+                nc.vector.tensor_scalar_add(y_sb[t][:, e * C : (e + 1) * C], acc[:], b_sb[:, t, e : e + 1])
+            else:
+                nc.scalar.activation(y_sb[t][:, e * C : (e + 1) * C], acc[:], IDENTITY, bias=b_sb[:, t, e : e + 1])
+
+        def load_b():
+            b_rows = b.rearrange("(g t r) e -> r g t e", t=4, r=8)
+            for r in range(8):
+                nc.gpsimd.dma_start(b_sb[r:P:8], b_rows[r])
+
+        def load_wp():
+            wp_rows = wp.rearrange("(g t r) f -> r g t f", t=4, r=8)
+            for r in range(8):
+                nc.sync.dma_start(wp_raw[r:P:8], wp_rows[r])
+
+        def prepare_wp():
+            nc.scalar.copy(wp_b[:].rearrange("p (f t) -> p f t", t=4), wp_raw[:].rearrange("p t f -> p f t"))
+            for c0, c1 in ((0, 256), (256, 384)):
+                nc.vector.quantize_mx(out=wp_w[:, c0:c1].bitcast(FP8X4), scales=wp_s[:, c0:c1], in_=wp_b[:, 4 * c0 : 4 * c1])
+
+        def fetch(t):
+            for i in range(2):
+                nc.vector.tensor_tensor(parts[i][:, t, :], y_sb[t][:].indirect(pos_sb[i][:]), gate_sb[i][:], MULT)
+
+        def fetch_half(t, i, h):
+            cols = slice(h * H, (h + 1) * H)
+            lists = pos_sb[i][:, h * 16 : (h + 1) * 16]
+            nc.vector.tensor_tensor(parts[i][:, t, cols], y_sb[t][:].indirect(lists), gate_sb[i][:, cols], MULT)
+
+        def combine(h):
+            cols = slice(h * H, (h + 1) * H)
+            c_b = keep.tile([P, H * 4], BF16, name="c_b", bufs=2, align_bytes=64)
+            nc.vector.tensor_tensor(
+                c_b[:].rearrange("p (c t) -> p c t", t=4),
+                parts[0][:, :, cols].rearrange("p t c -> p c t"),
+                parts[1][:, :, cols].rearrange("p t c -> p c t"),
+                ADD,
+            )
+            return c_b
+
+        def project(h, c_b):
+            cols = slice(h * H, (h + 1) * H)
+            c_w = keep.tile([P, H], U32, name="c_w", bufs=2, align_bytes=64)
+            c_s = keep.tile([P, H], U8, name="c_s", bufs=2, align_bytes=64)
+            nc.vector.quantize_mx(out=c_w[:].bitcast(FP8X4), scales=c_s[:], in_=c_b[:])
+            for f in range(3):
+                o_sb = keep.tile([P, H], F32, name="o_sb", bufs=6)
+                o_ps = psum.tile([P, H], F32, name="o_ps", bufs=3)
+                nc.tensor.matmul_mx(
+                    out=o_ps[:],
+                    lhsT=wp_w[:, f * P : (f + 1) * P].bitcast(FP8X4),
+                    lhsT_scale=wp_s[:, f * P : (f + 1) * P],
+                    rhs=c_w[:].bitcast(FP8X4),
+                    rhs_scale=c_s[:],
+                    start=True,
+                    stop=True,
+                )
+                if h == 1 and f != 1:
+                    nc.vector.tensor_copy(o_sb[:], o_ps[:])
+                else:
+                    nc.scalar.copy(o_sb[:], o_ps[:])
+                nc.sync.dma_start(out[f * P : (f + 1) * P, cols], o_sb[:])
+
+        nc.vector.memset(x_s[:].bitcast(I32), 0)
+        nc.vector.memset(ws_raw[:].bitcast(I32), 0)
+        load_b()
+        nc.sync.dma_start(offs_sb[:], offs)
+        load_x(0, 0)
+        load_x(0, 1)
+        load_x(1, 0)
+        load_x(1, 1)
+        load_w_scales()
+        load_x(2, 0)
+        load_x(2, 1)
+        for e in range(E):
+            load_w(e)
+
+        cast_x(0, 0, "v")
+        cast_x(0, 1, "v")
+        quantize_x(0)
+        cast_x(1, 0, "s")
+        cast_x(1, 1, "s")
+        for e in range(E):
+            permute_w(e, nc.gpsimd)
+        for e in range(E):
+            gather(0, e)
+        cast_x(2, 0, "s")
+        cast_x(2, 1, "v")
+        quantize_x(2)
+        quantize_x(1)
+        for e in range(E):
+            gather_scales(e)
+        permute_scales()
+        shift_scales(0, E, nc.sync)
+        for i in range(2):
+            nc.sync.dma_start(gate_sb[i][:], gate[i, 0:P, :])
+        nc.sync.dma_start(pos_sb[0][:], pos1)
+        nc.sync.dma_start(pos_sb[1][:], pos2)
+        load_wp()
+        for e in range(E):
+            gather(1, e)
+            gather(2, e)
+        for t in range(4):
+            for e in range(E):
+                expert(e, t)
+        prepare_wp()
+        for t in range(3):
+            fetch(t)
+        fetch_half(3, 0, 0)
+        fetch_half(3, 1, 0)
+        fetch_half(3, 0, 1)
+        c_0 = combine(0)
+        fetch_half(3, 1, 1)
+        project(0, c_0)
+        c_1 = combine(1)
+        project(1, c_1)

@@ -33,11 +33,11 @@ def tile_moe_nxt_lin_bias_kernel(tc, xT, w_words, w_scales, b, wp, gate, offs, p
         offs_sb = keep.tile([P, S // 16], U16, name="offs_sb")
         pos_sb = [keep.tile([P, T // 16], U16, name="pos_sb%d" % i) for i in range(2)]
 
-        x_raw = [[keep.tile([P, 4, H], F32, name="x_raw%d_%d" % (a, h)) for h in range(2)] for a in range(A)]
+        x_raw = [keep.tile([P, 4, T], F32, name="x_raw%d" % a) for a in range(A)]
         x_b = [keep.tile([P, T * 4], BF16, name="x_b%d" % a, align_bytes=64) for a in range(A)]
         x_w = [keep.tile([P, T], U32, name="x_w%d" % a, align_bytes=64) for a in range(A)]
         x_s = keep.tile([P, T], U8, name="x_s", align_bytes=64)
-        g_w = [keep.tile([P, A * C], U32, name="g_w%d" % e, align_bytes=64) for e in range(E)]
+        g_w = [keep.tile([P, S], U32, name="g_w%d" % a, align_bytes=64) for a in range(A)]
         g_s = keep.tile([P, S], U8, name="g_s", align_bytes=64)
         sh_s = [keep.tile([P, S], U8, name="sh_s%d" % a, align_bytes=64) for a in range(1, A)]
         w_raw = [keep.tile([P, A * 2 * N], U8, name="w_raw%d" % e, align_bytes=64) for e in range(E)]
@@ -53,9 +53,8 @@ def tile_moe_nxt_lin_bias_kernel(tc, xT, w_words, w_scales, b, wp, gate, offs, p
         y_sb = [keep.tile([P, S], F32, name="y_sb%d" % t) for t in range(4)]
         parts = [keep.tile([P, 4, T], F32, name="part%d" % i) for i in range(2)]
 
-        def load_x(a, h):
-            src = xT[a * 512 : (a + 1) * 512, h * H : (h + 1) * H]
-            nc.sync.dma_start(x_raw[a][h][:], src.rearrange("(p j) t -> p j t", j=4))
+        def load_x(a):
+            nc.sync.dma_start(x_raw[a][:], xT[a * 512 : (a + 1) * 512, :].rearrange("(p j) t -> p j t", j=4))
 
         def load_w(e):
             nc.sync.dma_start(
@@ -71,35 +70,26 @@ def tile_moe_nxt_lin_bias_kernel(tc, xT, w_words, w_scales, b, wp, gate, offs, p
                     scales[4 * q : 4 * q + 4],
                 )
 
-        def cast_x(a, h, engine):
-            dst = x_b[a][:, h * 1024 : (h + 1) * 1024].rearrange("p (t j) -> p t j", j=4)
-            src = x_raw[a][h][:].rearrange("p j t -> p t j")
-            if engine == "v":
-                nc.vector.tensor_copy(dst, src)
-            else:
-                nc.scalar.copy(dst, src)
+        def cast_x(a, c0, c1, copy):
+            dst = x_b[a][:, 4 * c0 : 4 * c1].rearrange("p (c i j) -> p c j i", i=4, j=4)
+            src = x_raw[a][:, :, c0:c1].rearrange("p j (c i) -> p c j i", i=4)
+            copy(dst, src)
 
         def quantize_x(a):
             nc.vector.quantize_mx(out=x_w[a][:].bitcast(FP8X4), scales=x_s[4 * a : P, :], in_=x_b[a][:])
 
-        def permute_w(e, engine):
-            dst = w_per[e][:].bitcast(I32).rearrange("p (a t q r) -> p a t q r", a=A, t=4, q=16)
-            src = w_raw[e][:].bitcast(I32).rearrange("p (a q t r) -> p a t q r", a=A, t=4, q=16)
-            for a in range(A):
-                engine.tensor_copy(dst[:, a], src[:, a])
+        def permute_w(e):
+            dst = w_per[e][:].bitcast(I32).rearrange("p (t aq r) -> p t aq r", t=4, r=4)
+            src = w_raw[e][:].bitcast(I32).rearrange("p (aq t r) -> p t aq r", t=4, r=4)
+            nc.vector.tensor_copy(dst, src)
 
         def permute_scales():
-            dst = ws_per[:].bitcast(I32).rearrange("p (c t q r) -> p t c q r", c=E * A, t=4, q=16)
-            src = ws_raw[:].bitcast(I32).rearrange("p (c q t r) -> p t c q r", c=E * A, t=4, q=16)
-            for t in range(4):
-                nc.vector.tensor_copy(dst[:, t], src[:, t])
+            dst = ws_per[:].bitcast(I32).rearrange("p (t c r) -> p t c r", t=4, r=2)
+            src = ws_raw[:].bitcast(I32).rearrange("p (c t r) -> p t c r", t=4, r=2)
+            nc.vector.tensor_copy(dst, src)
 
-        def gather(a, e):
-            lists = offs_sb[:, e * 16 : (e + 1) * 16]
-            nc.vector.tensor_copy(g_w[e][:, a * C : (a + 1) * C], x_w[a][:].indirect(lists))
-
-        def gather_scales(e):
-            nc.vector.tensor_copy(g_s[:, e * C : (e + 1) * C], x_s[:].indirect(offs_sb[:, e * 16 : (e + 1) * 16]))
+        def gather(dst, src, s0, s1):
+            nc.vector.tensor_copy(dst[:, s0:s1], src[:].indirect(offs_sb[:, s0 // 16 : s1 // 16]))
 
         def shift_scales(e0, e1, queue):
             for a in range(1, A):
@@ -113,19 +103,18 @@ def tile_moe_nxt_lin_bias_kernel(tc, xT, w_words, w_scales, b, wp, gate, offs, p
             acc = psum.tile([P, C], F32, name="acc", bufs=5)
             for h in range(2):
                 for a in range(A):
-                    c0 = a * C + h * 128
-                    s0 = (e * A + a) * N + t * 128
+                    s0 = (t * E * A + e * A + a) * 128
                     g0 = e * C + h * 128
                     nc.tensor.matmul_mx(
                         out=acc[:, h * 128 : (h + 1) * 128],
-                        lhsT=w_per[e][:, (a * 4 + t) * 256 : (a * 4 + t + 1) * 256].bitcast(FP4X4),
+                        lhsT=w_per[e][:, (t * A + a) * 256 : (t * A + a + 1) * 256].bitcast(FP4X4),
                         lhsT_scale=ws_per[:, s0 : s0 + 128],
-                        rhs=g_w[e][:, c0 : c0 + 128].bitcast(FP8X4),
+                        rhs=g_w[a][:, g0 : g0 + 128].bitcast(FP8X4),
                         rhs_scale=(g_s if a == 0 else sh_s[a - 1])[:, g0 : g0 + 128],
                         start=(a == 0),
                         stop=(a == A - 1),
                     )
-            if t == 0 and e % 2 == 1:
+            if t == 0 and e == 3:
                 nc.vector.tensor_scalar_add(y_sb[t][:, e * C : (e + 1) * C], acc[:], b_sb[:, t, e : e + 1])
             else:
                 nc.scalar.activation(y_sb[t][:, e * C : (e + 1) * C], acc[:], IDENTITY, bias=b_sb[:, t, e : e + 1])
@@ -141,7 +130,7 @@ def tile_moe_nxt_lin_bias_kernel(tc, xT, w_words, w_scales, b, wp, gate, offs, p
                 nc.sync.dma_start(wp_raw[r:P:8], wp_rows[r])
 
         def prepare_wp():
-            nc.scalar.copy(wp_b[:].rearrange("p (f t) -> p f t", t=4), wp_raw[:].rearrange("p t f -> p f t"))
+            nc.scalar.copy(wp_b[:].rearrange("p (c i t) -> p c t i", i=4, t=4), wp_raw[:].rearrange("p t (c i) -> p c t i", i=4))
             for c0, c1 in ((0, 256), (256, 384)):
                 nc.vector.quantize_mx(out=wp_w[:, c0:c1].bitcast(FP8X4), scales=wp_s[:, c0:c1], in_=wp_b[:, 4 * c0 : 4 * c1])
 
@@ -158,9 +147,9 @@ def tile_moe_nxt_lin_bias_kernel(tc, xT, w_words, w_scales, b, wp, gate, offs, p
             cols = slice(h * H, (h + 1) * H)
             c_b = keep.tile([P, H * 4], BF16, name="c_b", bufs=2, align_bytes=64)
             nc.vector.tensor_tensor(
-                c_b[:].rearrange("p (c t) -> p c t", t=4),
-                parts[0][:, :, cols].rearrange("p t c -> p c t"),
-                parts[1][:, :, cols].rearrange("p t c -> p c t"),
+                c_b[:].rearrange("p (c i t) -> p c t i", i=4, t=4),
+                parts[0][:, :, cols].rearrange("p t (c i) -> p c t i", i=4),
+                parts[1][:, :, cols].rearrange("p t (c i) -> p c t i", i=4),
                 ADD,
             )
             return c_b
@@ -188,35 +177,31 @@ def tile_moe_nxt_lin_bias_kernel(tc, xT, w_words, w_scales, b, wp, gate, offs, p
                     nc.scalar.copy(o_sb[:], o_ps[:])
                 nc.sync.dma_start(out[f * P : (f + 1) * P, cols], o_sb[:])
 
-        nc.vector.memset(x_s[:].bitcast(I32), 0)
+        CUTS = ((0, 384), (384, 768), (768, 1024))
         nc.vector.memset(ws_raw[:].bitcast(I32), 0)
+        nc.vector.memset(x_s[:].bitcast(I32), 0)
         load_b()
+        load_x(0)
         nc.sync.dma_start(offs_sb[:], offs)
-        load_x(0, 0)
-        load_x(0, 1)
-        load_x(1, 0)
-        load_x(1, 1)
+        load_x(1)
         load_w_scales()
-        load_x(2, 0)
-        load_x(2, 1)
+        load_x(2)
         for e in range(E):
             load_w(e)
 
-        cast_x(0, 0, "v")
-        cast_x(0, 1, "v")
+        cast_x(0, 0, 320, nc.vector.tensor_copy)
+        cast_x(0, 320, 512, nc.scalar.copy)
         quantize_x(0)
-        cast_x(1, 0, "s")
-        cast_x(1, 1, "s")
-        for e in range(E):
-            permute_w(e, nc.gpsimd)
-        for e in range(E):
-            gather(0, e)
-        cast_x(2, 0, "s")
-        cast_x(2, 1, "v")
-        quantize_x(2)
+        for s0, s1 in CUTS:
+            gather(g_w[0], x_w[0], s0, s1)
+        cast_x(1, 0, 384, nc.scalar.copy)
+        cast_x(1, 384, 512, nc.vector.tensor_copy)
         quantize_x(1)
-        for e in range(E):
-            gather_scales(e)
+        cast_x(2, 0, 256, nc.scalar.copy)
+        cast_x(2, 256, 512, nc.vector.tensor_copy)
+        quantize_x(2)
+        for s0, s1 in CUTS:
+            gather(g_s, x_s, s0, s1)
         permute_scales()
         shift_scales(0, E, nc.sync)
         for i in range(2):
@@ -224,9 +209,14 @@ def tile_moe_nxt_lin_bias_kernel(tc, xT, w_words, w_scales, b, wp, gate, offs, p
         nc.sync.dma_start(pos_sb[0][:], pos1)
         nc.sync.dma_start(pos_sb[1][:], pos2)
         load_wp()
-        for e in range(E):
-            gather(1, e)
-            gather(2, e)
+        for e in range(2):
+            permute_w(e)
+        for s0, s1 in CUTS:
+            for a in range(1, A):
+                gather(g_w[a], x_w[a], s0, s1)
+            if s0 == 0:
+                for e in range(2, E):
+                    permute_w(e)
         for t in range(4):
             for e in range(E):
                 expert(e, t)

@@ -53,8 +53,9 @@ def tile_moe_nxt_lin_bias_kernel(tc, xT, w_words, w_scales, b, wp, gate, offs, p
         y_sb = [keep.tile([P, S], F32, name="y_sb%d" % t) for t in range(4)]
         parts = [keep.tile([P, 4, T], F32, name="part%d" % i) for i in range(2)]
 
-        def load_x(a):
-            nc.sync.dma_start(x_raw[a][:], xT[a * 512 : (a + 1) * 512, :].rearrange("(p j) t -> p j t", j=4))
+        def load_x(a, j0=0, j1=4):
+            rows = xT[a * 512 : (a + 1) * 512, :].rearrange("(p j) t -> p j t", j=4)
+            nc.sync.dma_start(x_raw[a][:, j0:j1, :], rows[:, j0:j1, :])
 
         def load_w(e):
             nc.sync.dma_start(
@@ -70,9 +71,9 @@ def tile_moe_nxt_lin_bias_kernel(tc, xT, w_words, w_scales, b, wp, gate, offs, p
                     scales[4 * q : 4 * q + 4],
                 )
 
-        def cast_x(a, c0, c1, copy):
-            dst = x_b[a][:, 4 * c0 : 4 * c1].rearrange("p (c i j) -> p c j i", i=4, j=4)
-            src = x_raw[a][:, :, c0:c1].rearrange("p j (c i) -> p c j i", i=4)
+        def cast_x(a, copy, c0=0, c1=T, j0=0, j1=4):
+            dst = x_b[a][:, 4 * c0 : 4 * c1].rearrange("p (c i j) -> p c j i", i=4, j=4)[:, :, j0:j1, :]
+            src = x_raw[a][:, j0:j1, c0:c1].rearrange("p j (c i) -> p c j i", i=4)
             copy(dst, src)
 
         def quantize_x(a):
@@ -100,7 +101,7 @@ def tile_moe_nxt_lin_bias_kernel(tc, xT, w_words, w_scales, b, wp, gate, offs, p
                     )
 
         def expert(e, t):
-            acc = psum.tile([P, C], F32, name="acc", bufs=5)
+            acc = psum.tile([P, C], F32, name="acc", bufs=4)
             for h in range(2):
                 for a in range(A):
                     s0 = (t * E * A + e * A + a) * 128
@@ -119,10 +120,23 @@ def tile_moe_nxt_lin_bias_kernel(tc, xT, w_words, w_scales, b, wp, gate, offs, p
             else:
                 nc.scalar.activation(y_sb[t][:, e * C : (e + 1) * C], acc[:], IDENTITY, bias=b_sb[:, t, e : e + 1])
 
+        def warm_up():
+            warm = psum.tile([P, 512], F32, name="warm")
+            for i in range(6):
+                nc.tensor.matmul_mx(
+                    out=warm[:],
+                    lhsT=w_per[0][:, 0:256].bitcast(FP4X4),
+                    lhsT_scale=ws_per[:, 0:128],
+                    rhs=g_w[0][:, 0:512].bitcast(FP8X4),
+                    rhs_scale=g_s[:, 0:512],
+                    start=True,
+                    stop=True,
+                )
+
         def load_b():
             b_rows = b.rearrange("(g t r) e -> r g t e", t=4, r=8)
             for r in range(8):
-                nc.gpsimd.dma_start(b_sb[r:P:8], b_rows[r])
+                nc.sync.dma_start(b_sb[r:P:8], b_rows[r])
 
         def load_wp():
             wp_rows = wp.rearrange("(g t r) f -> r g t f", t=4, r=8)
@@ -178,45 +192,49 @@ def tile_moe_nxt_lin_bias_kernel(tc, xT, w_words, w_scales, b, wp, gate, offs, p
                 nc.sync.dma_start(out[f * P : (f + 1) * P, cols], o_sb[:])
 
         CUTS = ((0, 384), (384, 768), (768, 1024))
+        scopy = nc.scalar.copy
+        vcopy = nc.vector.tensor_copy
         nc.vector.memset(ws_raw[:].bitcast(I32), 0)
         nc.vector.memset(x_s[:].bitcast(I32), 0)
-        load_b()
-        load_x(0)
+        load_x(0, 0, 2)
+        load_x(0, 2, 4)
         nc.sync.dma_start(offs_sb[:], offs)
         load_x(1)
         load_w_scales()
         load_x(2)
         for e in range(E):
             load_w(e)
+        load_b()
+        load_wp()
+        nc.sync.dma_start(pos_sb[0][:], pos1)
+        nc.sync.dma_start(pos_sb[1][:], pos2)
 
-        cast_x(0, 0, 320, nc.vector.tensor_copy)
-        cast_x(0, 320, 512, nc.scalar.copy)
+        cast_x(0, vcopy, j0=0, j1=2)
+        cast_x(0, vcopy, c0=0, c1=288, j0=2, j1=4)
+        cast_x(0, scopy, c0=288, c1=512, j0=2, j1=4)
         quantize_x(0)
         for s0, s1 in CUTS:
             gather(g_w[0], x_w[0], s0, s1)
-        cast_x(1, 0, 384, nc.scalar.copy)
-        cast_x(1, 384, 512, nc.vector.tensor_copy)
+        cast_x(1, scopy)
         quantize_x(1)
-        cast_x(2, 0, 256, nc.scalar.copy)
-        cast_x(2, 256, 512, nc.vector.tensor_copy)
+        cast_x(2, scopy)
         quantize_x(2)
         for s0, s1 in CUTS:
             gather(g_s, x_s, s0, s1)
-        permute_scales()
         shift_scales(0, E, nc.sync)
         for i in range(2):
             nc.sync.dma_start(gate_sb[i][:], gate[i, 0:P, :])
-        nc.sync.dma_start(pos_sb[0][:], pos1)
-        nc.sync.dma_start(pos_sb[1][:], pos2)
-        load_wp()
-        for e in range(2):
-            permute_w(e)
-        for s0, s1 in CUTS:
+        permute_w(0)
+        permute_w(1)
+        permute_scales()
+        for a in range(1, A):
+            gather(g_w[a], x_w[a], 0, 384)
+        permute_w(2)
+        permute_w(3)
+        for s0, s1 in CUTS[1:]:
             for a in range(1, A):
                 gather(g_w[a], x_w[a], s0, s1)
-            if s0 == 0:
-                for e in range(2, E):
-                    permute_w(e)
+        warm_up()
         for t in range(4):
             for e in range(E):
                 expert(e, t)

@@ -72,8 +72,8 @@ def tile_moe_nxt_lin_bias_kernel(tc, xT, w_words, w_scales, b, wp, gate, offs, p
                 )
 
         def cast_x(a, copy, c0=0, c1=T, j0=0, j1=4):
-            dst = x_b[a][:, 4 * c0 : 4 * c1].rearrange("p (c i j) -> p c j i", i=4, j=4)[:, :, j0:j1, :]
-            src = x_raw[a][:, j0:j1, c0:c1].rearrange("p j (c i) -> p c j i", i=4)
+            dst = x_b[a][:, 4 * c0 : 4 * c1].rearrange("p (t j) -> p t j", j=4)[:, :, j0:j1]
+            src = x_raw[a][:, j0:j1, c0:c1].rearrange("p j t -> p t j")
             copy(dst, src)
 
         def quantize_x(a):
@@ -125,8 +125,8 @@ def tile_moe_nxt_lin_bias_kernel(tc, xT, w_words, w_scales, b, wp, gate, offs, p
             for i in range(6):
                 nc.tensor.matmul_mx(
                     out=warm[:],
-                    lhsT=w_per[0][:, 0:256].bitcast(FP4X4),
-                    lhsT_scale=ws_per[:, 0:128],
+                    lhsT=w_raw[0][:, 0:256].bitcast(FP4X4),
+                    lhsT_scale=ws_raw[:, 0:128],
                     rhs=g_w[0][:, 0:512].bitcast(FP8X4),
                     rhs_scale=g_s[:, 0:512],
                     start=True,
@@ -136,7 +136,7 @@ def tile_moe_nxt_lin_bias_kernel(tc, xT, w_words, w_scales, b, wp, gate, offs, p
         def load_b():
             b_rows = b.rearrange("(g t r) e -> r g t e", t=4, r=8)
             for r in range(8):
-                nc.sync.dma_start(b_sb[r:P:8], b_rows[r])
+                nc.gpsimd.dma_start(b_sb[r:P:8], b_rows[r])
 
         def load_wp():
             wp_rows = wp.rearrange("(g t r) f -> r g t f", t=4, r=8)
@@ -144,7 +144,7 @@ def tile_moe_nxt_lin_bias_kernel(tc, xT, w_words, w_scales, b, wp, gate, offs, p
                 nc.sync.dma_start(wp_raw[r:P:8], wp_rows[r])
 
         def prepare_wp():
-            nc.scalar.copy(wp_b[:].rearrange("p (c i t) -> p c t i", i=4, t=4), wp_raw[:].rearrange("p t (c i) -> p c t i", i=4))
+            nc.scalar.copy(wp_b[:].rearrange("p (f t) -> p f t", t=4), wp_raw[:].rearrange("p t f -> p f t"))
             for c0, c1 in ((0, 256), (256, 384)):
                 nc.vector.quantize_mx(out=wp_w[:, c0:c1].bitcast(FP8X4), scales=wp_s[:, c0:c1], in_=wp_b[:, 4 * c0 : 4 * c1])
 
@@ -196,18 +196,19 @@ def tile_moe_nxt_lin_bias_kernel(tc, xT, w_words, w_scales, b, wp, gate, offs, p
         vcopy = nc.vector.tensor_copy
         nc.vector.memset(ws_raw[:].bitcast(I32), 0)
         nc.vector.memset(x_s[:].bitcast(I32), 0)
+        load_b()
         load_x(0, 0, 2)
         load_x(0, 2, 4)
         nc.sync.dma_start(offs_sb[:], offs)
         load_x(1)
-        load_w_scales()
         load_x(2)
         for e in range(E):
             load_w(e)
-        load_b()
-        load_wp()
+        load_w_scales()
         nc.sync.dma_start(pos_sb[0][:], pos1)
         nc.sync.dma_start(pos_sb[1][:], pos2)
+        for i in range(2):
+            nc.sync.dma_start(gate_sb[i][:], gate[i, 0:P, :])
 
         cast_x(0, vcopy, j0=0, j1=2)
         cast_x(0, vcopy, c0=0, c1=288, j0=2, j1=4)
@@ -217,18 +218,18 @@ def tile_moe_nxt_lin_bias_kernel(tc, xT, w_words, w_scales, b, wp, gate, offs, p
             gather(g_w[0], x_w[0], s0, s1)
         cast_x(1, scopy)
         quantize_x(1)
-        cast_x(2, scopy)
+        cast_x(2, scopy, c0=0, c1=416)
+        cast_x(2, vcopy, c0=416, c1=512)
         quantize_x(2)
         for s0, s1 in CUTS:
             gather(g_s, x_s, s0, s1)
         shift_scales(0, E, nc.sync)
-        for i in range(2):
-            nc.sync.dma_start(gate_sb[i][:], gate[i, 0:P, :])
+        load_wp()
         permute_w(0)
         permute_w(1)
-        permute_scales()
         for a in range(1, A):
             gather(g_w[a], x_w[a], 0, 384)
+        permute_scales()
         permute_w(2)
         permute_w(3)
         for s0, s1 in CUTS[1:]:

from contextlib import ExitStack

import concourse.mybir as mybir

K, T, E, C, N, M = 1536, 512, 4, 256, 512, 384
P = 128
A = K // 512
S = E * C
H = T // 2

F32 = mybir.dt.float32
BF16 = mybir.dt.bfloat16
I32 = mybir.dt.int32
U32 = mybir.dt.uint32
U16 = mybir.dt.uint16
U8 = mybir.dt.uint8
FP8X4 = mybir.dt.float8_e4m3fn_x4
FP4X4 = mybir.dt.float4_e2m1fn_x4
MULT = mybir.AluOpType.mult
ADD = mybir.AluOpType.add
IDENTITY = mybir.ActivationFunctionType.Identity

FLOPS = 2 * K * N * S + 2 * N * M * T
BYTES = 4 * K * T + E * K * N // 2 + E * K * N // 32 + 4 * N * E + 4 * N * M + 8 * T + 2 * P * 128 + 4 * M * T


def tile_moe_nxt_lin_bias_kernel(tc, xT, w_words, w_scales, b, wp, gate, offs, pos1, pos2, out):
    nc = tc.nc
    with ExitStack() as ctx:
        keep = ctx.enter_context(tc.tile_pool(name="keep", bufs=1))
        psum = ctx.enter_context(tc.psum_pool(name="psum", bufs=1))

        offs_sb = keep.tile([P, S // 16], U16, name="offs_sb")
        pos_sb = [keep.tile([P, T // 16], U16, name="pos_sb%d" % i) for i in range(2)]

        x_raw = [keep.tile([P, 4, T], F32, name="x_raw%d" % a) for a in range(A)]
        x_b = [keep.tile([P, T * 4], BF16, name="x_b%d" % a, align_bytes=64) for a in range(A)]
        x_w = [keep.tile([P, T], U32, name="x_w%d" % a, align_bytes=64) for a in range(A)]
        x_s = keep.tile([P, T], U8, name="x_s", align_bytes=64)
        g_w = [keep.tile([P, S], U32, name="g_w%d" % a, align_bytes=64) for a in range(A)]
        g_s = keep.tile([P, S], U8, name="g_s", align_bytes=64)
        sh_s = [keep.tile([P, S], U8, name="sh_s%d" % a, align_bytes=64) for a in range(1, A)]
        w_raw = [keep.tile([P, A * 2 * N], U8, name="w_raw%d" % e, align_bytes=64) for e in range(E)]
        w_per = [keep.tile([P, A * 2 * N], U8, name="w_per%d" % e, align_bytes=64) for e in range(E)]
        ws_raw = keep.tile([P, E * A * N], U8, name="ws_raw", align_bytes=64)
        ws_per = keep.tile([P, E * A * N], U8, name="ws_per", align_bytes=64)
        b_sb = keep.tile([P, 4, E], F32, name="b_sb")
        wp_raw = keep.tile([P, 4, M], F32, name="wp_raw")
        wp_b = keep.tile([P, M * 4], BF16, name="wp_b", align_bytes=64)
        wp_w = keep.tile([P, M], U32, name="wp_w", align_bytes=64)
        wp_s = keep.tile([P, M], U8, name="wp_s", align_bytes=64)
        gate_sb = [keep.tile([P, T], F32, name="gate_sb%d" % i) for i in range(2)]
        y_sb = [keep.tile([P, S], F32, name="y_sb%d" % t) for t in range(4)]
        parts = [keep.tile([P, 4, T], F32, name="part%d" % i) for i in range(2)]

        def load_x(a, j0=0, j1=4):
            rows = xT[a * 512 : (a + 1) * 512, :].rearrange("(p j) t -> p j t", j=4)
            nc.sync.dma_start(x_raw[a][:, j0:j1, :], rows[:, j0:j1, :])

        def load_w(e):
            nc.sync.dma_start(
                w_raw[e][:].bitcast(I32).rearrange("p (a n) -> p a n", a=A),
                w_words[e].bitcast(I32).rearrange("a p n -> p a n"),
            )

        def load_w_scales():
            scales = w_scales.bitcast(I32).rearrange("e a q n -> q (e a) n")
            for q in range(4):
                nc.sync.dma_start(
                    ws_raw[32 * q : 32 * q + 4, :].bitcast(I32).rearrange("q (c n) -> q c n", n=N // 4),
                    scales[4 * q : 4 * q + 4],
                )

        def cast_x(a, copy, c0=0, c1=T, j0=0, j1=4):
            dst = x_b[a][:, 4 * c0 : 4 * c1].rearrange("p (t j) -> p t j", j=4)[:, :, j0:j1]
            src = x_raw[a][:, j0:j1, c0:c1].rearrange("p j t -> p t j")
            copy(dst, src)

        def quantize_x(a):
            nc.vector.quantize_mx(out=x_w[a][:].bitcast(FP8X4), scales=x_s[4 * a : P, :], in_=x_b[a][:])

        def permute_w(e):
            dst = w_per[e][:].bitcast(I32).rearrange("p (t aq r) -> p t aq r", t=4, r=4)
            src = w_raw[e][:].bitcast(I32).rearrange("p (aq t r) -> p t aq r", t=4, r=4)
            nc.vector.tensor_copy(dst, src)

        def permute_scales():
            dst = ws_per[:].bitcast(I32).rearrange("p (t c r) -> p t c r", t=4, r=2)
            src = ws_raw[:].bitcast(I32).rearrange("p (c t r) -> p t c r", t=4, r=2)
            nc.vector.tensor_copy(dst, src)

        def gather(dst, src, s0, s1):
            nc.vector.tensor_copy(dst[:, s0:s1], src[:].indirect(offs_sb[:, s0 // 16 : s1 // 16]))

        def shift_scales(e0, e1, queue):
            for a in range(1, A):
                for q in range(4):
                    queue.dma_start(
                        sh_s[a - 1][32 * q : 32 * q + 4, e0 * C : e1 * C].bitcast(I32),
                        g_s[32 * q + 4 * a : 32 * q + 4 * a + 4, e0 * C : e1 * C].bitcast(I32),
                    )

        def expert(e, t):
            acc = psum.tile([P, C], F32, name="acc", bufs=4)
            for h in range(2):
                for a in range(A):
                    s0 = (t * E * A + e * A + a) * 128
                    g0 = e * C + h * 128
                    nc.tensor.matmul_mx(
                        out=acc[:, h * 128 : (h + 1) * 128],
                        lhsT=w_per[e][:, (t * A + a) * 256 : (t * A + a + 1) * 256].bitcast(FP4X4),
                        lhsT_scale=ws_per[:, s0 : s0 + 128],
                        rhs=g_w[a][:, g0 : g0 + 128].bitcast(FP8X4),
                        rhs_scale=(g_s if a == 0 else sh_s[a - 1])[:, g0 : g0 + 128],
                        start=(a == 0),
                        stop=(a == A - 1),
                    )
            if t == 0 and e == 3:
                nc.vector.tensor_scalar_add(y_sb[t][:, e * C : (e + 1) * C], acc[:], b_sb[:, t, e : e + 1])
            else:
                nc.scalar.activation(y_sb[t][:, e * C : (e + 1) * C], acc[:], IDENTITY, bias=b_sb[:, t, e : e + 1])

        def warm_up():
            warm = psum.tile([P, 512], F32, name="warm")
            for i in range(6):
                nc.tensor.matmul_mx(
                    out=warm[:],
                    lhsT=w_raw[0][:, 0:256].bitcast(FP4X4),
                    lhsT_scale=ws_raw[:, 0:128],
                    rhs=g_w[0][:, 0:512].bitcast(FP8X4),
                    rhs_scale=g_s[:, 0:512],
                    start=True,
                    stop=True,
                )

        def load_b():
            b_rows = b.rearrange("(g t r) e -> r g t e", t=4, r=8)
            for r in range(8):
                nc.gpsimd.dma_start(b_sb[r:P:8], b_rows[r])

        def load_wp():
            wp_rows = wp.rearrange("(g t r) f -> r g t f", t=4, r=8)
            for r in range(8):
                nc.sync.dma_start(wp_raw[r:P:8], wp_rows[r])

        def prepare_wp():
            nc.scalar.copy(wp_b[:].rearrange("p (f t) -> p f t", t=4), wp_raw[:].rearrange("p t f -> p f t"))
            for c0, c1 in ((0, 256), (256, 384)):
                nc.vector.quantize_mx(out=wp_w[:, c0:c1].bitcast(FP8X4), scales=wp_s[:, c0:c1], in_=wp_b[:, 4 * c0 : 4 * c1])

        def fetch(t):
            for i in range(2):
                nc.vector.tensor_tensor(parts[i][:, t, :], y_sb[t][:].indirect(pos_sb[i][:]), gate_sb[i][:], MULT)

        def fetch_half(t, i, h):
            cols = slice(h * H, (h + 1) * H)
            lists = pos_sb[i][:, h * 16 : (h + 1) * 16]
            nc.vector.tensor_tensor(parts[i][:, t, cols], y_sb[t][:].indirect(lists), gate_sb[i][:, cols], MULT)

        def combine(h):
            cols = slice(h * H, (h + 1) * H)
            c_b = keep.tile([P, H * 4], BF16, name="c_b", bufs=2, align_bytes=64)
            nc.vector.tensor_tensor(
                c_b[:].rearrange("p (c i t) -> p c t i", i=4, t=4),
                parts[0][:, :, cols].rearrange("p t (c i) -> p c t i", i=4),
                parts[1][:, :, cols].rearrange("p t (c i) -> p c t i", i=4),
                ADD,
            )
            return c_b

        def project(h, c_b):
            cols = slice(h * H, (h + 1) * H)
            c_w = keep.tile([P, H], U32, name="c_w", bufs=2, align_bytes=64)
            c_s = keep.tile([P, H], U8, name="c_s", bufs=2, align_bytes=64)
            nc.vector.quantize_mx(out=c_w[:].bitcast(FP8X4), scales=c_s[:], in_=c_b[:])
            for f in range(3):
                o_sb = keep.tile([P, H], F32, name="o_sb", bufs=6)
                o_ps = psum.tile([P, H], F32, name="o_ps", bufs=3)
                nc.tensor.matmul_mx(
                    out=o_ps[:],
                    lhsT=wp_w[:, f * P : (f + 1) * P].bitcast(FP8X4),
                    lhsT_scale=wp_s[:, f * P : (f + 1) * P],
                    rhs=c_w[:].bitcast(FP8X4),
                    rhs_scale=c_s[:],
                    start=True,
                    stop=True,
                )
                if h == 1 and f != 1:
                    nc.vector.tensor_copy(o_sb[:], o_ps[:])
                else:
                    nc.scalar.copy(o_sb[:], o_ps[:])
                nc.sync.dma_start(out[f * P : (f + 1) * P, cols], o_sb[:])

        CUTS = ((0, 384), (384, 768), (768, 1024))
        scopy = nc.scalar.copy
        vcopy = nc.vector.tensor_copy
        nc.vector.memset(ws_raw[:].bitcast(I32), 0)
        nc.vector.memset(x_s[:].bitcast(I32), 0)
        load_b()
        load_x(0, 0, 2)
        load_x(0, 2, 4)
        nc.sync.dma_start(offs_sb[:], offs)
        load_x(1)
        load_x(2)
        for e in range(E):
            load_w(e)
        load_w_scales()
        nc.sync.dma_start(pos_sb[0][:], pos1)
        nc.sync.dma_start(pos_sb[1][:], pos2)
        for i in range(2):
            nc.sync.dma_start(gate_sb[i][:], gate[i, 0:P, :])

        cast_x(0, vcopy, j0=0, j1=2)
        cast_x(0, vcopy, c0=0, c1=288, j0=2, j1=4)
        cast_x(0, scopy, c0=288, c1=512, j0=2, j1=4)
        quantize_x(0)
        for s0, s1 in CUTS:
            gather(g_w[0], x_w[0], s0, s1)
        cast_x(1, scopy)
        quantize_x(1)
        cast_x(2, scopy, c0=0, c1=416)
        cast_x(2, vcopy, c0=416, c1=512)
        quantize_x(2)
        for s0, s1 in CUTS:
            gather(g_s, x_s, s0, s1)
        shift_scales(0, E, nc.sync)
        load_wp()
        permute_w(0)
        permute_w(1)
        for a in range(1, A):
            gather(g_w[a], x_w[a], 0, 384)
        permute_scales()
        permute_w(2)
        permute_w(3)
        for s0, s1 in CUTS[1:]:
            for a in range(1, A):
                gather(g_w[a], x_w[a], s0, s1)
        warm_up()
        for t in range(4):
            for e in range(E):
                expert(e, t)
        prepare_wp()
        for t in range(3):
            fetch(t)
        fetch_half(3, 0, 0)
        fetch_half(3, 1, 0)
        fetch_half(3, 0, 1)
        c_0 = combine(0)
        fetch_half(3, 1, 1)
        project(0, c_0)
        c_1 = combine(1)
        project(1, c_1)
